import numpy as np
import ml_dtypes


def mxq(x, axis, fmt="e4m3"):
    dtype, down = {"e4m3": (ml_dtypes.float8_e4m3fn, 7), "e5m2": (ml_dtypes.float8_e5m2, 14)}[fmt]
    v = np.moveaxis(np.asarray(x, np.float32).astype(ml_dtypes.bfloat16).astype(np.float64), axis, -1)
    blocks = v.reshape(v.shape[:-1] + (-1, 32))
    amax = np.abs(blocks).max(-1, keepdims=True)
    byte = np.maximum(np.where(amax > 0, np.frexp(amax)[1] - 1 + 127, 0) - down, 1)
    scale = np.exp2(byte - 127.0)
    codes = (blocks / scale).astype(np.float32).astype(dtype).astype(np.float64)
    return np.moveaxis((codes * scale).reshape(v.shape), -1, axis)


WIDE = False


def mx_kscale(k):
    if not WIDE:
        return np.ones(k)
    levels = np.array([10, -10, 5, -5, 0])
    if k % 512:
        return np.exp2(np.random.permutation(np.resize(levels, k // 32))).repeat(32)
    a = np.empty((k // 512, 16))
    for p in range(k // 512):
        a[p, :8] = np.random.permutation(np.resize(levels, 8))
        for g in range(8):
            far = levels[np.abs(levels - a[p, g]) >= 10]
            a[p, g + 8] = far[np.random.randint(len(far))]
    return np.exp2(a.ravel()).repeat(32)


def f64(x):
    return np.asarray(x).astype(np.float64)


def striped(idx):
    return np.tile(idx.reshape(-1, 16).T, (8, 1)).astype(np.uint16)


def unstriped(offs):
    return offs[:16].T.reshape(-1).astype(np.int64)


E2M1 = np.array([0.0, 0.5, 1.0, 1.5, 2.0, 3.0, 4.0, 6.0, -0.0, -0.5, -1.0, -1.5, -2.0, -3.0, -4.0, -6.0])


def pack_weight(w, fmt):
    k, n = w.shape
    w = f64(np.asarray(w, np.float32).astype(ml_dtypes.bfloat16)).reshape(k // 32, 32, n)
    amax = np.abs(w).max(1)
    if fmt == "e4m3":
        byte = np.frexp(amax)[1] - 1 + 127 - 7
    else:
        mant, ex = np.frexp(amax / 6.0)
        byte = np.where(mant > 0.5, ex, ex - 1) + 127
    byte = np.clip(np.where(amax > 0, byte, 1), 1, 254)
    scaled = (w * np.exp2(127.0 - byte)[:, None, :]).reshape(k, n).astype(np.float32)
    by_word = np.ascontiguousarray(scaled.reshape(k // 512, 128, 4, n).transpose(0, 1, 3, 2))
    if fmt == "e4m3":
        words = by_word.astype(ml_dtypes.float8_e4m3fn).view(np.uint8)
    else:
        c = by_word.astype(ml_dtypes.float4_e2m1fn).view(np.uint8) & 0xF
        words = (c[..., 0::2] | (c[..., 1::2] << 4)).reshape(k // 512, 128, 2 * n)
    return np.ascontiguousarray(words), np.ascontiguousarray(byte.astype(np.uint8).reshape(k // 512, 16, n))


def unpack_weight(words, scales, fmt):
    g, _, n = scales.shape
    words = np.ascontiguousarray(words).reshape(g, 128, n, -1)
    if fmt == "e4m3":
        vals = words.view(ml_dtypes.float8_e4m3fn).astype(np.float64)
    else:
        nib = np.empty((g, 128, n, 4), np.uint8)
        nib[..., 0::2] = words & 0xF
        nib[..., 1::2] = words >> 4
        vals = E2M1[nib]
    vals = vals * np.repeat(np.exp2(scales.astype(np.float64) - 127.0), 8, axis=1)[..., None]
    return vals.transpose(0, 1, 3, 2).reshape(g * 512, n)


def gelu(v):
    return 0.5 * v * (1.0 + np.tanh(np.sqrt(2.0 / np.pi) * (v + 0.044715 * v**3)))


def bf(x):
    return np.asarray(x, np.float32).astype(ml_dtypes.bfloat16)


def planes(Y):
    n, m = Y.shape
    b = f64(bf(Y)).reshape(n // 32, 32, m)
    amax = np.abs(b).max(1)
    byte = np.clip(np.where(amax > 0, np.frexp(amax)[1] - 1 + 127 - 7, 1), 1, 254)
    codes = (b * np.exp2(127.0 - byte)[:, None, :]).reshape(n, m).astype(np.float32).astype(ml_dtypes.float8_e4m3fn).view(np.uint8)
    words = codes.reshape(n // 512, 128, 4, m).transpose(0, 1, 3, 2)
    return np.ascontiguousarray(words), np.ascontiguousarray(byte.astype(np.uint8).reshape(n // 512, 16, m))


K, K2, H, N, T, TB, S, P = 512, 1024, 1024, 512, 4096, 2048, 1024, 512

def setup_inputs():
    n = np.random.standard_normal
    s = mx_kscale(K)[:, None]
    s2 = mx_kscale(K2)[:, None]
    u = mx_kscale(H)[:, None]
    d = {}
    d["tab_words"], d["tab_scales"] = pack_weight(n((K, T)) * s, "e4m3")
    d["tab2_words"], d["tab2_scales"] = pack_weight(n((K2, TB)) * s2, "e4m3")
    d["offs"] = striped(np.random.permutation(T)[:S])
    d["offs2"] = striped(np.random.permutation(TB)[:P])
    d["pos1"] = striped(np.random.permutation(S)[:P])
    d["w1"] = (0.47 * n((K, H)) / K**0.5 / s).astype(np.float32)
    d["w2_words"], d["w2_scales"] = pack_weight(n((K2, H)) / K2**0.5 / s2, "e2m1")
    d["gain"] = (0.17 * np.random.uniform(0.7, 1.3, H)).astype(np.float32)
    d["wgs"] = np.exp(0.3 * n((128, P))).astype(np.float32)
    d["gz"] = (np.random.uniform(0.6, 1.4, H) * u[:, 0]).astype(np.float32)
    w3 = 1.5 * n((H, N)) / H**0.5 / u * np.exp(0.8 * n(N))[None, :]
    d["w3_words"], d["w3_scales"] = pack_weight(w3, "e4m3")
    return d

def reference(tab_words, tab_scales, tab2_words, tab2_scales, offs, offs2, pos1, w1, w2_words, w2_scales, gain, wgs, gz, w3_words, w3_scales):
    v = unpack_weight(tab_words, tab_scales, "e4m3")[:, unstriped(offs)]
    v2 = unpack_weight(tab2_words, tab2_scales, "e4m3")[:, unstriped(offs2)]
    w2 = unpack_weight(w2_words, w2_scales, "e2m1")
    w3 = unpack_weight(w3_words, w3_scales, "e4m3")
    a = mxq(f64(w1), 0, "e4m3").T @ v
    b = (w2.T @ v2) * f64(gain)[:, None]
    placed = np.zeros((H, S))
    placed[:, unstriped(pos1)] = np.tile(f64(wgs), (H // 128, 1)) * b
    z = f64(gz)[:, None] * (np.sin(a + placed) + placed)
    y = w3.T @ mxq(z, 0, "e4m3")
    words, scales = planes(y)
    return y, words, scales

@@ -1,0 +1,328 @@
+import math
+from contextlib import ExitStack
+
+import concourse.mybir as mybir
+
+F32 = mybir.dt.float32
+BF16 = mybir.dt.bfloat16
+I32 = mybir.dt.int32
+U32 = mybir.dt.uint32
+U16 = mybir.dt.uint16
+U8 = mybir.dt.uint8
+FP8X4 = mybir.dt.float8_e4m3fn_x4
+FP4X4 = mybir.dt.float4_e2m1fn_x4
+ALU = mybir.AluOpType
+ACT = mybir.ActivationFunctionType
+
+P = 128
+T, TB, S, PM = 4096, 2048, 1024, 512
+FLOPS = 3221225472
+WINDOWS = 2
+HALF = 512
+QUART = 256
+
+
+def tile_list_trapeze_timing_features_kernel(
+    tc, tab_words, tab_scales, tab2_words, tab2_scales, offs, offs2, pos1, w1, w2_words, w2_scales,
+    gain, wgs, gz, w3_words, w3_scales, out_0, out_1, out_2,
+):
+    nc = tc.nc
+    with ExitStack() as ctx:
+        lists = ctx.enter_context(tc.tile_pool(name="lists", bufs=1))
+        keep = ctx.enter_context(tc.tile_pool(name="keep", bufs=1))
+        ring = ctx.enter_context(tc.tile_pool(name="ring", bufs=3))
+        psum = ctx.enter_context(tc.psum_pool(name="psum", bufs=1))
+
+        def held(shape, dtype, name, after=""):
+            return keep.tile(shape, dtype, name=name, tag=after or name, align_bytes=64)
+
+        def bank(shape, k):
+            return psum.tile(shape, F32, name="bank%d" % k, tag="bank%d" % k)
+
+        idx = lists.tile([P, S // 16], U16, name="idx")
+        idx2 = lists.tile([P, PM // 16], U16, name="idx2")
+        place = lists.tile([P, PM // 16], U16, name="place")
+
+        tab2_s = held([P, 2, TB], U8, "tab2_s")
+        w2_s_raw = held([P, 2, 1024], U8, "w2_s_raw")
+        tab_s = held([P, T], U8, "tab_s")
+        w3_s_raw = held([P, 512], U8, "w3_s_raw")
+        nc.gpsimd.memset(w2_s_raw[:].bitcast(I32), 0)
+        nc.vector.memset(tab2_s[:].bitcast(I32), 0)
+        nc.vector.memset(tab_s[:].bitcast(I32), 0)
+        nc.vector.memset(w3_s_raw[:].bitcast(I32), 0)
+        neg_half_pi = held([P, 1], F32, "neg_half_pi")
+        neg_pi = held([P, 1], F32, "neg_pi")
+        with tc.tile_pool(name="early", bufs=1) as early:
+            ones = early.tile([P, 1], F32, name="ones")
+            nc.vector.memset(ones[:], 1.0)
+            nc.vector.tensor_scalar(out=neg_half_pi[:], in0=ones[:], scalar1=-math.pi / 2, scalar2=None, op0=ALU.mult)
+            nc.vector.tensor_scalar(out=neg_pi[:], in0=ones[:], scalar1=-math.pi, scalar2=None, op0=ALU.mult)
+        late = ctx.enter_context(tc.tile_pool(name="late", bufs=1))
+        windows = [held([P, S], F32, "window0")]
+        nc.vector.memset(windows[0][:], 0.0)
+
+        def load_scale_rows(queue, tile, scales, packed):
+            words = scales.bitcast(I32)
+            passes = scales.shape[0]
+            for q in range(4):
+                rows = words[:, 4 * q : 4 * q + 4, :]
+                if packed:
+                    queue.dma_start(out=tile[32 * q : 32 * q + 4 * passes, :].bitcast(I32), in_=rows)
+                elif passes == 1:
+                    queue.dma_start(out=tile[32 * q : 32 * q + 4, :].bitcast(I32), in_=rows[0])
+                else:
+                    queue.dma_start(out=tile[32 * q : 32 * q + 4, :, :].bitcast(I32), in_=rows.rearrange("a r c -> r a c"))
+
+        w2_raw = held([P, 2, 2048], U8, "w2_raw")
+        tab2_w = [held([P, TB], I32, "tab2_w0"), held([P, TB], I32, "tab2_w1")]
+        tab_w = late.tile([P, T], I32, name="tab_w", tag="tab_w", align_bytes=64)
+        w1_raw = [late.tile([P, 4, 512], F32, name="w1_raw%d" % b) for b in range(2)]
+        wg = [late.tile([P, 2, PM], F32, name="wg%d" % u) for u in range(2)]
+        w3_raw = late.tile([P, 2, 512], I32, name="w3_raw")
+        gain_sb = late.tile([P, 2, 4], F32, name="gain_sb")
+        gz_sb = late.tile([P, 2, 4], F32, name="gz_sb")
+        w1_rows = w1.rearrange("(p j) r -> p j r", j=4)
+        wgs_rows = wgs.rearrange("(i t) j -> i t j", t=4)
+
+        def load_wgs(u):
+            for q in (0, 2, 1, 3):
+                nc.sync.dma_start(out=wg[u][32 * q : 32 * q + 32, :, :], in_=wgs_rows[:, 2 * u : 2 * u + 2, :])
+
+        nc.sync.dma_start(out=idx2[:], in_=offs2)
+        nc.sync.dma_start(out=place[:], in_=pos1)
+        nc.sync.dma_start(out=idx[:], in_=offs)
+        nc.sync.dma_start(out=w2_raw[:].bitcast(I32), in_=w2_words.bitcast(I32).rearrange("a p c -> p a c"))
+        load_scale_rows(nc.scalar, tab2_s, tab2_scales, False)
+        load_scale_rows(nc.gpsimd, w2_s_raw, w2_scales, False)
+        for a in range(2):
+            nc.sync.dma_start(out=tab2_w[a][:], in_=tab2_words[a].rearrange("p t i -> p (t i)").bitcast(I32))
+        nc.sync.dma_start(out=gain_sb[:], in_=gain.rearrange("(b p t) -> p b t", b=2, t=4))
+        nc.sync.dma_start(out=gz_sb[:], in_=gz.rearrange("(b p t) -> p b t", b=2, t=4))
+        load_wgs(0)
+        load_scale_rows(nc.sync, tab_s, tab_scales, False)
+        nc.sync.dma_start(out=w1_raw[0][:], in_=w1_rows[:, :, 0:512])
+        nc.sync.dma_start(out=tab_w[:], in_=tab_words[0].rearrange("p t i -> p (t i)").bitcast(I32))
+        load_wgs(1)
+        nc.sync.dma_start(out=w1_raw[1][:], in_=w1_rows[:, :, 512:1024])
+        load_scale_rows(nc.sync, w3_s_raw, w3_scales, True)
+        nc.sync.dma_start(out=w3_raw[:], in_=w3_words.rearrange("a p n i -> p a (n i)").bitcast(I32))
+
+
+        w2_d = [held([P, 2, 1024], U8, "w2_d%d" % b) for b in range(2)]
+        w2_s = [held([P, 2, 512], U8, "w2_s%d" % b) for b in range(2)]
+
+        def deal_w2(b):
+            nc.scalar.copy(
+                out=w2_d[b][:].bitcast(U16).rearrange("p a (t c i) -> p a c t i", t=4, i=8),
+                in_=w2_raw[:].bitcast(U16)[:, :, 512 * b : 512 * b + 512].rearrange("p a (c i t) -> p a c t i", t=4, i=8),
+            )
+            nc.vector.tensor_copy(
+                out=w2_s[b][:].rearrange("p a (t c i) -> p a c t i", t=4, i=16),
+                in_=w2_s_raw[:, :, 512 * b : 512 * b + 512].rearrange("p a (c i t) -> p a c t i", t=4, i=16),
+            )
+
+        v2 = [held([P, PM], I32, "v2_%d" % a) for a in range(2)]
+        v2_s = held([P, 2, PM], U8, "v2_s")
+        deal_w2(0)
+        for a in range(2):
+            nc.vector.tensor_copy(out=v2_s[:, a, :], in_=tab2_s[:, a, :].indirect(idx2[:]))
+        nc.vector.tensor_copy(out=v2[0][:].bitcast(U32), in_=tab2_w[0][:].bitcast(U32).indirect(idx2[:]))
+        deal_w2(1)
+
+        gz8 = gz_sb[:].rearrange("p b t -> p (b t)")
+        gain_gz = held([P, 8], F32, "gain_gz")
+        safe_gz = held([P, 8], F32, "safe_gz")
+        inv_gz = held([P, 8], F32, "inv_gz")
+        nc.vector.tensor_tensor(out=gain_gz[:], in0=gain_sb[:].rearrange("p b t -> p (b t)"), in1=gz8, op=ALU.mult)
+        nc.vector.scalar_tensor_tensor(out=safe_gz[:], in0=gz8, scalar=0.0, in1=gz8, op0=ALU.is_equal, op1=ALU.add)
+        nc.vector.tensor_copy(out=v2[1][:].bitcast(U32), in_=tab2_w[1][:].bitcast(U32).indirect(idx2[:]))
+        nc.vector.reciprocal(out=inv_gz[:], in_=safe_gz[:])
+
+        offsets = []
+
+        def timing_offsets(i):
+            b, t = divmod(i, 4)
+            acc = bank([P, PM], i % 4)
+            for a in range(2):
+                nc.tensor.matmul_mx(
+                    out=acc[:], lhsT=w2_d[b][:, a, 256 * t : 256 * t + 256].bitcast(FP4X4),
+                    lhsT_scale=w2_s[b][:, a, 128 * t : 128 * t + 128],
+                    rhs=v2[a][:].bitcast(FP8X4), rhs_scale=v2_s[:, a, :], start=(a == 0), stop=(a == 1),
+                )
+            scaled = held([P, PM], F32, "offset%d" % i)
+            nc.scalar.activation(out=scaled[:], in_=acc[:], func=ACT.Copy, scale=gain_gz[:, i : i + 1])
+            offsets.append(scaled)
+
+        def scatter(i):
+            t = i % 4
+            nc.vector.tensor_tensor(
+                out=windows[i % WINDOWS][:].indirect(place[:]), in0=offsets[i][:], in1=wg[t // 2][:, t % 2, :], op=ALU.mult
+            )
+
+        v_s = held([P, S], U8, "v_s")
+        v = [held([P, HALF], I32, "v%d" % h) for h in range(2)]
+        w1_q = [held([P, 512], I32, "w1_q%d" % b) for b in range(2)]
+        w1_s = [held([P, 512], U8, "w1_s%d" % b) for b in range(2)]
+        w1_bf = []
+
+        def round_w1(b):
+            w1_bf.append(held([P, 2048], BF16, "w1_bf%d" % b, after="offset2" if b == 1 else ""))
+            nc.scalar.copy(
+                out=w1_bf[b][:].rearrange("p (t m j) -> p m t j", t=4, j=4),
+                in_=w1_raw[b][:].rearrange("p j (m t) -> p m t j", t=4),
+            )
+
+        def quantize_w1(b):
+            nc.vector.quantize_mx(out=w1_q[b][:].bitcast(FP8X4), scales=w1_s[b][:], in_=w1_bf[b][:])
+
+        timing_offsets(0)
+        scatter(0)
+        round_w1(0)
+        for i in range(1, 8):
+            timing_offsets(i)
+        nc.vector.tensor_copy(out=v_s[:], in_=tab_s[:].indirect(idx[:]))
+        quantize_w1(0)
+        for h in range(2):
+            nc.vector.tensor_copy(out=v[h][:].bitcast(U32), in_=tab_w[:].bitcast(U32).indirect(idx[:, 32 * h : 32 * h + 32]))
+        windows.append(late.tile([P, S], F32, name="window1", tag="tab_w", align_bytes=64))
+        nc.gpsimd.memset(windows[1][:], 0.0)
+
+        def deal_w3():
+            w3_d = held([P, 2, 512], I32, "w3_d", after="offset4")
+            w3_s = held([P, 512], U8, "w3_s", after="offset3")
+            nc.scalar.copy(
+                out=w3_d[:].bitcast(U32).rearrange("p a (t c i) -> p a c t i", t=4, i=4),
+                in_=w3_raw[:].bitcast(U32).rearrange("p a (c i t) -> p a c t i", t=4, i=4),
+            )
+            nc.vector.tensor_copy(
+                out=w3_s[:].rearrange("p (t c i) -> p c t i", t=4, i=16),
+                in_=w3_s_raw[:].rearrange("p (c i t) -> p c t i", t=4, i=16),
+            )
+            return w3_d, w3_s
+
+        width = (HALF, QUART)
+        z_rows = [[held([P, 4, width[b]], BF16, "z_rows%d_%d" % (b, c)) for c in range(S // width[b])] for b in range(2)]
+        z_q = [[held([P, width[b]], I32, "z_q%d_%d" % (b, c)) for c in range(S // width[b])] for b in range(2)]
+        z_s = [[held([P, width[b]], U8, "z_s%d_%d" % (b, c)) for c in range(S // width[b])] for b in range(2)]
+        sines = {}
+
+        def phases(i):
+            b, t = divmod(i, 4)
+            step = QUART if i == 7 else HALF
+            xs = []
+            for h in range(2):
+                acc = bank([P, HALF], 4 + (2 * i + h) % 4)
+                nc.tensor.matmul_mx(
+                    out=acc[:], lhsT=w1_q[b][:, 128 * t : 128 * t + 128].bitcast(FP8X4),
+                    lhsT_scale=w1_s[b][:, 128 * t : 128 * t + 128],
+                    rhs=v[h][:].bitcast(FP8X4), rhs_scale=v_s[:, HALF * h : HALF * h + HALF], start=True, stop=True,
+                )
+                for c0 in range(0, HALF, step):
+                    x = ring.tile([P, step], F32, name="x", tag="x", bufs=4)
+                    j0 = HALF * h + c0
+                    nc.vector.scalar_tensor_tensor(
+                        out=x[:], in0=windows[i % WINDOWS][:, j0 : j0 + step], scalar=inv_gz[:, i : i + 1],
+                        in1=acc[:, c0 : c0 + step], op0=ALU.mult, op1=ALU.add,
+                    )
+                    xs.append((j0, x))
+            for pair in range(0, len(xs), 2):
+                two = xs[pair : pair + 2]
+                once, twice = [], []
+                for j0, x in two:
+                    f = ring.tile([P, step], F32, name="fold1", tag="fold1", bufs=2)
+                    nc.scalar.activation(out=f[:], in_=x[:], func=ACT.Abs, bias=neg_half_pi[:])
+                    once.append(f)
+                for f in once:
+                    g = ring.tile([P, step], F32, name="fold2", tag="fold2", bufs=2)
+                    nc.scalar.activation(out=g[:], in_=f[:], func=ACT.Abs, bias=neg_pi[:])
+                    twice.append(g)
+                for (j0, x), g in zip(two, twice):
+                    s = ring.tile([P, step], F32, name="sine", tag="sine", bufs=6)
+                    nc.scalar.activation(out=s[:], in_=g[:], func=ACT.Sin, bias=neg_half_pi[:])
+                    sines[(i, j0)] = (s, step)
+
+        def finish(i, c):
+            b, t = divmod(i, 4)
+            w = width[b]
+            j0 = w * c
+            base = j0 if (i, j0) in sines else j0 - QUART
+            s = sines[(i, base)][0]
+            nc.vector.scalar_tensor_tensor(
+                out=z_rows[b][c][:, t, :], in0=s[:, j0 - base : j0 - base + w], scalar=gz8[:, i : i + 1],
+                in1=windows[i % WINDOWS][:, j0 : j0 + w], op0=ALU.mult, op1=ALU.add,
+            )
+
+        def quantize_z(b, c):
+            w = width[b]
+            woven = ring.tile([P, 4 * w], BF16, name="z_woven", tag="z_woven", bufs=2, align_bytes=64)
+            dst = woven[:].rearrange("p (c i t) -> p c t i", t=4, i=4)
+            src = z_rows[b][c][:].rearrange("p t (c i) -> p c t i", i=4)
+            if b == 0:
+                nc.scalar.copy(out=dst, in_=src)
+            else:
+                nc.vector.tensor_copy(out=dst, in_=src)
+            nc.vector.quantize_mx(out=z_q[b][c][:].bitcast(FP8X4), scales=z_s[b][c][:], in_=woven[:])
+
+        y_banks = {}
+
+        def y_pass(a, q):
+            c, c0 = divmod(QUART * q, width[a])
+            for t in range(4):
+                u = t // 2
+                if a == 0 and t % 2 == 0:
+                    y_banks[(q, u)] = bank([P, 2, QUART], 2 * q + u)
+                nc.tensor.matmul_mx(
+                    out=y_banks[(q, u)][:, t % 2, :], lhsT=w3_d[:, a, 128 * t : 128 * t + 128].bitcast(FP8X4),
+                    lhsT_scale=w3_s[4 * a : 128, 128 * t : 128 * t + 128],
+                    rhs=z_q[a][c][:, c0 : c0 + QUART].bitcast(FP8X4), rhs_scale=z_s[a][c][:, c0 : c0 + QUART],
+                    start=(a == 0 and t % 2 == 0), stop=(a == 1 and t % 2 == 1),
+                )
+
+        y_s = held([P, S], U8, "y_s")
+        out_rows = out_0.rearrange("(p t) j -> p t j", t=4)
+        out_words = out_1[0].rearrange("p m t -> p (m t)").bitcast(I32)
+
+        def hand_out(q):
+            cols = slice(QUART * q, QUART * q + QUART)
+            y = held([P, 4, QUART], F32, "y%d" % q)
+            for u in range(2):
+                nc.scalar.copy(out=y[:, 2 * u : 2 * u + 2, :], in_=y_banks[(q, u)][:])
+            nc.sync.dma_start(out=out_rows[:, :, cols], in_=y[:])
+            woven = ring.tile([P, 4 * QUART], BF16, name="y_woven", tag="y_woven", bufs=2, align_bytes=64)
+            weave = nc.vector.tensor_copy if q % 2 == 0 else nc.scalar.copy
+            weave(out=woven[:].rearrange("p (c i t) -> p c t i", t=4, i=4), in_=y[:].rearrange("p t (c i) -> p c t i", i=4))
+            y_q = held([P, QUART], I32, "y_q%d" % q)
+            nc.vector.quantize_mx(out=y_q[:].bitcast(FP8X4), scales=y_s[:, cols], in_=woven[:])
+            nc.sync.dma_start(out=out_words[:, cols], in_=y_q[:])
+
+        for i in range(8):
+            phases(i)
+            if i >= 1:
+                for c in range(len(z_rows[(i - 1) // 4])):
+                    finish(i - 1, c)
+            if i + 1 < 8:
+                scatter(i + 1)
+            if i == 1:
+                round_w1(1)
+            if i == 2:
+                quantize_w1(1)
+            if i == 3:
+                w3_d, w3_s = deal_w3()
+            if i == 4:
+                for h in range(2):
+                    quantize_z(0, h)
+                for q in range(2):
+                    y_pass(0, q)
+        for q in range(2, 4):
+            y_pass(0, q)
+        for q in range(4):
+            finish(7, q)
+            quantize_z(1, q)
+            y_pass(1, q)
+            if q >= 1:
+                hand_out(q - 1)
+        hand_out(3)
+        scale_words = out_2[0].bitcast(I32)
+        for q in range(4):
+            nc.sync.dma_start(out=scale_words[4 * q : 4 * q + 4, :], in_=y_s[32 * q : 32 * q + 4, :].bitcast(I32))

@@ -20,6 +20,7 @@ FLOPS = 3221225472
 WINDOWS = 2
 HALF = 512
 QUART = 256
+EIGHTH = 128
 
 
 def tile_list_trapeze_timing_features_kernel(
@@ -47,18 +48,22 @@ def tile_list_trapeze_timing_features_kernel(
         w2_s_raw = held([P, 2, 1024], U8, "w2_s_raw")
         tab_s = held([P, T], U8, "tab_s")
         w3_s_raw = held([P, 512], U8, "w3_s_raw")
-        nc.gpsimd.memset(w2_s_raw[:].bitcast(I32), 0)
-        nc.vector.memset(tab2_s[:].bitcast(I32), 0)
-        nc.vector.memset(tab_s[:].bitcast(I32), 0)
-        nc.vector.memset(w3_s_raw[:].bitcast(I32), 0)
         neg_half_pi = held([P, 1], F32, "neg_half_pi")
         neg_pi = held([P, 1], F32, "neg_pi")
-        with tc.tile_pool(name="early", bufs=1) as early:
-            ones = early.tile([P, 1], F32, name="ones")
-            nc.vector.memset(ones[:], 1.0)
-            nc.vector.tensor_scalar(out=neg_half_pi[:], in0=ones[:], scalar1=-math.pi / 2, scalar2=None, op0=ALU.mult)
-            nc.vector.tensor_scalar(out=neg_pi[:], in0=ones[:], scalar1=-math.pi, scalar2=None, op0=ALU.mult)
+
+        def constant(tile, value, name):
+            with tc.tile_pool(name=name, bufs=1) as early:
+                ones = early.tile([P, 1], F32, name="ones")
+                nc.vector.memset(ones[:], 1.0)
+                nc.vector.tensor_scalar(out=tile[:], in0=ones[:], scalar1=value, scalar2=None, op0=ALU.mult)
+
+        nc.gpsimd.memset(w2_s_raw[:].bitcast(I32), 0)
+        nc.vector.memset(tab2_s[:].bitcast(I32), 0)
+        constant(neg_half_pi, -math.pi / 2, "early")
         late = ctx.enter_context(tc.tile_pool(name="late", bufs=1))
+        nc.vector.memset(tab_s[:].bitcast(I32), 0)
+        constant(neg_pi, -math.pi, "early2")
+        last = ctx.enter_context(tc.tile_pool(name="last", bufs=1))
         windows = [held([P, S], F32, "window0")]
         nc.vector.memset(windows[0][:], 0.0)
 
@@ -74,12 +79,12 @@ def tile_list_trapeze_timing_features_kernel(
                 else:
                     queue.dma_start(out=tile[32 * q : 32 * q + 4, :, :].bitcast(I32), in_=rows.rearrange("a r c -> r a c"))
 
-        w2_raw = held([P, 2, 2048], U8, "w2_raw")
-        tab2_w = [held([P, TB], I32, "tab2_w0"), held([P, TB], I32, "tab2_w1")]
-        tab_w = late.tile([P, T], I32, name="tab_w", tag="tab_w", align_bytes=64)
-        w1_raw = [late.tile([P, 4, 512], F32, name="w1_raw%d" % b) for b in range(2)]
-        wg = [late.tile([P, 2, PM], F32, name="wg%d" % u) for u in range(2)]
-        w3_raw = late.tile([P, 2, 512], I32, name="w3_raw")
+        w2_raw = [late.tile([P, 2, 1024], U8, name="w2_raw%d" % b, align_bytes=64) for b in range(2)]
+        tab2_w = [late.tile([P, TB], I32, name="tab2_w%d" % a, align_bytes=64) for a in range(2)]
+        tab_w = last.tile([P, T], I32, name="tab_w", tag="tab_w", align_bytes=64)
+        w1_raw = [late.tile([P, 4, 512], F32, name="w1_raw0"), last.tile([P, 4, 512], F32, name="w1_raw1", tag="w1_raw1", align_bytes=64)]
+        wg = [late.tile([P, 2, PM], F32, name="wg0"), last.tile([P, 2, PM], F32, name="wg1")]
+        w3_raw = last.tile([P, 2, 512], I32, name="w3_raw")
         gain_sb = late.tile([P, 2, 4], F32, name="gain_sb")
         gz_sb = late.tile([P, 2, 4], F32, name="gz_sb")
         w1_rows = w1.rearrange("(p j) r -> p j r", j=4)
@@ -92,30 +97,34 @@ def tile_list_trapeze_timing_features_kernel(
         nc.sync.dma_start(out=idx2[:], in_=offs2)
         nc.sync.dma_start(out=place[:], in_=pos1)
         nc.sync.dma_start(out=idx[:], in_=offs)
-        nc.sync.dma_start(out=w2_raw[:].bitcast(I32), in_=w2_words.bitcast(I32).rearrange("a p c -> p a c"))
         load_scale_rows(nc.scalar, tab2_s, tab2_scales, False)
         load_scale_rows(nc.gpsimd, w2_s_raw, w2_scales, False)
-        for a in range(2):
-            nc.sync.dma_start(out=tab2_w[a][:], in_=tab2_words[a].rearrange("p t i -> p (t i)").bitcast(I32))
+        nc.gpsimd.memset(w3_s_raw[:].bitcast(I32), 0)
+        load_scale_rows(nc.gpsimd, w3_s_raw, w3_scales, True)
+        w2_rows = w2_words.bitcast(I32).rearrange("a p c -> p a c")
+        nc.sync.dma_start(out=tab2_w[0][:], in_=tab2_words[0].rearrange("p t i -> p (t i)").bitcast(I32))
+        nc.sync.dma_start(out=w2_raw[0][:].bitcast(I32), in_=w2_rows[:, :, 0:256])
+        nc.sync.dma_start(out=tab2_w[1][:], in_=tab2_words[1].rearrange("p t i -> p (t i)").bitcast(I32))
         nc.sync.dma_start(out=gain_sb[:], in_=gain.rearrange("(b p t) -> p b t", b=2, t=4))
         nc.sync.dma_start(out=gz_sb[:], in_=gz.rearrange("(b p t) -> p b t", b=2, t=4))
         load_wgs(0)
-        load_scale_rows(nc.sync, tab_s, tab_scales, False)
         nc.sync.dma_start(out=w1_raw[0][:], in_=w1_rows[:, :, 0:512])
+        nc.sync.dma_start(out=w2_raw[1][:].bitcast(I32), in_=w2_rows[:, :, 256:512])
+        load_scale_rows(nc.sync, tab_s, tab_scales, False)
         nc.sync.dma_start(out=tab_w[:], in_=tab_words[0].rearrange("p t i -> p (t i)").bitcast(I32))
         load_wgs(1)
         nc.sync.dma_start(out=w1_raw[1][:], in_=w1_rows[:, :, 512:1024])
-        load_scale_rows(nc.sync, w3_s_raw, w3_scales, True)
         nc.sync.dma_start(out=w3_raw[:], in_=w3_words.rearrange("a p n i -> p a (n i)").bitcast(I32))
 
 
         w2_d = [held([P, 2, 1024], U8, "w2_d%d" % b) for b in range(2)]
-        w2_s = [held([P, 2, 512], U8, "w2_s%d" % b) for b in range(2)]
+        w2_s = []
 
         def deal_w2(b):
+            w2_s.append(held([P, 2, 512], U8, "w2_s%d" % b, after=("tab2_s", "offset0")[b]))
             nc.scalar.copy(
                 out=w2_d[b][:].bitcast(U16).rearrange("p a (t c i) -> p a c t i", t=4, i=8),
-                in_=w2_raw[:].bitcast(U16)[:, :, 512 * b : 512 * b + 512].rearrange("p a (c i t) -> p a c t i", t=4, i=8),
+                in_=w2_raw[b][:].bitcast(U16).rearrange("p a (c i t) -> p a c t i", t=4, i=8),
             )
             nc.vector.tensor_copy(
                 out=w2_s[b][:].rearrange("p a (t c i) -> p a c t i", t=4, i=16),
@@ -124,11 +133,10 @@ def tile_list_trapeze_timing_features_kernel(
 
         v2 = [held([P, PM], I32, "v2_%d" % a) for a in range(2)]
         v2_s = held([P, 2, PM], U8, "v2_s")
-        deal_w2(0)
         for a in range(2):
             nc.vector.tensor_copy(out=v2_s[:, a, :], in_=tab2_s[:, a, :].indirect(idx2[:]))
         nc.vector.tensor_copy(out=v2[0][:].bitcast(U32), in_=tab2_w[0][:].bitcast(U32).indirect(idx2[:]))
-        deal_w2(1)
+        deal_w2(0)
 
         gz8 = gz_sb[:].rearrange("p b t -> p (b t)")
         gain_gz = held([P, 8], F32, "gain_gz")
@@ -150,7 +158,7 @@ def tile_list_trapeze_timing_features_kernel(
                     lhsT_scale=w2_s[b][:, a, 128 * t : 128 * t + 128],
                     rhs=v2[a][:].bitcast(FP8X4), rhs_scale=v2_s[:, a, :], start=(a == 0), stop=(a == 1),
                 )
-            scaled = held([P, PM], F32, "offset%d" % i)
+            scaled = held([P, PM], F32, "offset%d" % i, after="offset%d" % (0, 1, 2, 3, 1, 2, 3, 1)[i])
             nc.scalar.activation(out=scaled[:], in_=acc[:], func=ACT.Copy, scale=gain_gz[:, i : i + 1])
             offsets.append(scaled)
 
@@ -179,17 +187,18 @@ def tile_list_trapeze_timing_features_kernel(
         timing_offsets(0)
         scatter(0)
         round_w1(0)
-        for i in range(1, 8):
+        deal_w2(1)
+        for i in range(1, 3):
             timing_offsets(i)
         nc.vector.tensor_copy(out=v_s[:], in_=tab_s[:].indirect(idx[:]))
         quantize_w1(0)
         for h in range(2):
             nc.vector.tensor_copy(out=v[h][:].bitcast(U32), in_=tab_w[:].bitcast(U32).indirect(idx[:, 32 * h : 32 * h + 32]))
-        windows.append(late.tile([P, S], F32, name="window1", tag="tab_w", align_bytes=64))
+        windows.append(last.tile([P, S], F32, name="window1", tag="tab_w", align_bytes=64))
         nc.gpsimd.memset(windows[1][:], 0.0)
 
         def deal_w3():
-            w3_d = held([P, 2, 512], I32, "w3_d", after="offset4")
+            w3_d = last.tile([P, 2, 512], I32, name="w3_d", tag="w1_raw1", align_bytes=64)
             w3_s = held([P, 512], U8, "w3_s", after="offset3")
             nc.scalar.copy(
                 out=w3_d[:].bitcast(U32).rearrange("p a (t c i) -> p a c t i", t=4, i=4),
@@ -201,10 +210,12 @@ def tile_list_trapeze_timing_features_kernel(
             )
             return w3_d, w3_s
 
-        width = (HALF, QUART)
-        z_rows = [[held([P, 4, width[b]], BF16, "z_rows%d_%d" % (b, c)) for c in range(S // width[b])] for b in range(2)]
-        z_q = [[held([P, width[b]], I32, "z_q%d_%d" % (b, c)) for c in range(S // width[b])] for b in range(2)]
-        z_s = [[held([P, width[b]], U8, "z_s%d_%d" % (b, c)) for c in range(S // width[b])] for b in range(2)]
+        halves = [(0, HALF), (HALF, HALF)]
+        pieces = [(0, QUART), (QUART, QUART), (2 * QUART, QUART), (3 * QUART, EIGHTH), (3 * QUART + EIGHTH, EIGHTH)]
+        spans = (halves, pieces)
+        z_rows = [[held([P, 4, w], BF16, "z_rows%d_%d" % (b, j0)) for j0, w in spans[b]] for b in range(2)]
+        z_q = [[held([P, w], I32, "z_q%d_%d" % (b, j0)) for j0, w in spans[b]] for b in range(2)]
+        z_s = [[held([P, w], U8, "z_s%d_%d" % (b, j0)) for j0, w in spans[b]] for b in range(2)]
         sines = {}
 
         def phases(i):
@@ -240,61 +251,58 @@ def tile_list_trapeze_timing_features_kernel(
                 for (j0, x), g in zip(two, twice):
                     s = ring.tile([P, step], F32, name="sine", tag="sine", bufs=6)
                     nc.scalar.activation(out=s[:], in_=g[:], func=ACT.Sin, bias=neg_half_pi[:])
-                    sines[(i, j0)] = (s, step)
+                    sines[(i, j0 // step)] = s
 
         def finish(i, c):
             b, t = divmod(i, 4)
-            w = width[b]
-            j0 = w * c
-            base = j0 if (i, j0) in sines else j0 - QUART
-            s = sines[(i, base)][0]
+            j0, w = spans[b][c]
+            n, c0 = divmod(j0, QUART if i == 7 else HALF)
             nc.vector.scalar_tensor_tensor(
-                out=z_rows[b][c][:, t, :], in0=s[:, j0 - base : j0 - base + w], scalar=gz8[:, i : i + 1],
+                out=z_rows[b][c][:, t, :], in0=sines[(i, n)][:, c0 : c0 + w], scalar=gz8[:, i : i + 1],
                 in1=windows[i % WINDOWS][:, j0 : j0 + w], op0=ALU.mult, op1=ALU.add,
             )
 
-        def quantize_z(b, c):
-            w = width[b]
-            woven = ring.tile([P, 4 * w], BF16, name="z_woven", tag="z_woven", bufs=2, align_bytes=64)
-            dst = woven[:].rearrange("p (c i t) -> p c t i", t=4, i=4)
-            src = z_rows[b][c][:].rearrange("p t (c i) -> p c t i", i=4)
-            if b == 0:
-                nc.scalar.copy(out=dst, in_=src)
-            else:
-                nc.vector.tensor_copy(out=dst, in_=src)
+        def weave(copy, rows, w, tag):
+            woven = ring.tile([P, 4 * w], BF16, name=tag, tag=tag, bufs=3, align_bytes=64)
+            copy(out=woven[:].rearrange("p (c i t) -> p c t i", t=4, i=4), in_=rows[:].rearrange("p t (c i) -> p c t i", i=4))
+            return woven
+
+        def quantize_z(b, c, copy):
+            woven = weave(copy, z_rows[b][c], spans[b][c][1], "z_woven")
             nc.vector.quantize_mx(out=z_q[b][c][:].bitcast(FP8X4), scales=z_s[b][c][:], in_=woven[:])
 
         y_banks = {}
 
-        def y_pass(a, q):
-            c, c0 = divmod(QUART * q, width[a])
+        def y_pass(a, c):
+            j0, w = pieces[c]
+            per_bank = 512 // w
+            n, c0 = (c, 0) if a == 1 else divmod(j0, HALF)
             for t in range(4):
-                u = t // 2
-                if a == 0 and t % 2 == 0:
-                    y_banks[(q, u)] = bank([P, 2, QUART], 2 * q + u)
+                u, slot = divmod(t, per_bank)
+                if a == 0 and slot == 0:
+                    y_banks[(c, u)] = bank([P, per_bank, w], j0 // EIGHTH + u)
                 nc.tensor.matmul_mx(
-                    out=y_banks[(q, u)][:, t % 2, :], lhsT=w3_d[:, a, 128 * t : 128 * t + 128].bitcast(FP8X4),
+                    out=y_banks[(c, u)][:, slot, :], lhsT=w3_d[:, a, 128 * t : 128 * t + 128].bitcast(FP8X4),
                     lhsT_scale=w3_s[4 * a : 128, 128 * t : 128 * t + 128],
-                    rhs=z_q[a][c][:, c0 : c0 + QUART].bitcast(FP8X4), rhs_scale=z_s[a][c][:, c0 : c0 + QUART],
-                    start=(a == 0 and t % 2 == 0), stop=(a == 1 and t % 2 == 1),
+                    rhs=z_q[a][n][:, c0 : c0 + w].bitcast(FP8X4), rhs_scale=z_s[a][n][:, c0 : c0 + w],
+                    start=(a == 0 and slot == 0), stop=(a == 1 and slot == per_bank - 1),
                 )
 
         y_s = held([P, S], U8, "y_s")
         out_rows = out_0.rearrange("(p t) j -> p t j", t=4)
         out_words = out_1[0].rearrange("p m t -> p (m t)").bitcast(I32)
 
-        def hand_out(q):
-            cols = slice(QUART * q, QUART * q + QUART)
-            y = held([P, 4, QUART], F32, "y%d" % q)
-            for u in range(2):
-                nc.scalar.copy(out=y[:, 2 * u : 2 * u + 2, :], in_=y_banks[(q, u)][:])
-            nc.sync.dma_start(out=out_rows[:, :, cols], in_=y[:])
-            woven = ring.tile([P, 4 * QUART], BF16, name="y_woven", tag="y_woven", bufs=2, align_bytes=64)
-            weave = nc.vector.tensor_copy if q % 2 == 0 else nc.scalar.copy
-            weave(out=woven[:].rearrange("p (c i t) -> p c t i", t=4, i=4), in_=y[:].rearrange("p t (c i) -> p c t i", i=4))
-            y_q = held([P, QUART], I32, "y_q%d" % q)
-            nc.vector.quantize_mx(out=y_q[:].bitcast(FP8X4), scales=y_s[:, cols], in_=woven[:])
-            nc.sync.dma_start(out=out_words[:, cols], in_=y_q[:])
+        def hand_out(c, copy):
+            j0, w = pieces[c]
+            per_bank = 512 // w
+            y = held([P, 4, w], F32, "y%d" % c)
+            for u in range(4 // per_bank):
+                nc.scalar.copy(out=y[:, per_bank * u : per_bank * u + per_bank, :], in_=y_banks[(c, u)][:])
+            nc.sync.dma_start(out=out_rows[:, :, j0 : j0 + w], in_=y[:])
+            woven = weave(copy, y, w, "y_woven")
+            y_q = held([P, w], I32, "y_q%d" % c)
+            nc.vector.quantize_mx(out=y_q[:].bitcast(FP8X4), scales=y_s[:, j0 : j0 + w], in_=woven[:])
+            nc.sync.dma_start(out=out_words[:, j0 : j0 + w], in_=y_q[:])
 
         for i in range(8):
             phases(i)
@@ -307,22 +315,23 @@ def tile_list_trapeze_timing_features_kernel(
                 round_w1(1)
             if i == 2:
                 quantize_w1(1)
-            if i == 3:
-                w3_d, w3_s = deal_w3()
+            if i + 3 < 8:
+                timing_offsets(i + 3)
             if i == 4:
                 for h in range(2):
-                    quantize_z(0, h)
+                    quantize_z(0, h, nc.scalar.copy)
+            if i == 5:
+                w3_d, w3_s = deal_w3()
                 for q in range(2):
                     y_pass(0, q)
-        for q in range(2, 4):
-            y_pass(0, q)
-        for q in range(4):
-            finish(7, q)
-            quantize_z(1, q)
-            y_pass(1, q)
-            if q >= 1:
-                hand_out(q - 1)
-        hand_out(3)
+        for c in range(2, len(pieces)):
+            y_pass(0, c)
+        for c in range(len(pieces)):
+            finish(7, c)
+            quantize_z(1, c, nc.scalar.copy if c == 1 else nc.vector.tensor_copy)
+            y_pass(1, c)
+        for c in range(len(pieces)):
+            hand_out(c, nc.scalar.copy if c == 0 else nc.vector.tensor_copy)
         scale_words = out_2[0].bitcast(I32)
         for q in range(4):
             nc.sync.dma_start(out=scale_words[4 * q : 4 * q + 4, :], in_=y_s[32 * q : 32 * q + 4, :].bitcast(I32))

@@ -17,7 +17,7 @@ ACT = mybir.ActivationFunctionType
 P = 128
 T, TB, S, PM = 4096, 2048, 1024, 512
 FLOPS = 3221225472
-WINDOWS = 2
+WINDOWS = 3
 HALF = 512
 QUART = 256
 EIGHTH = 128
@@ -64,8 +64,9 @@ def tile_list_trapeze_timing_features_kernel(
         nc.vector.memset(tab_s[:].bitcast(I32), 0)
         constant(neg_pi, -math.pi, "early2")
         last = ctx.enter_context(tc.tile_pool(name="last", bufs=1))
-        windows = [held([P, S], F32, "window0")]
+        windows = [held([P, S], F32, "window0"), held([P, S], F32, "window1")]
         nc.vector.memset(windows[0][:], 0.0)
+        nc.vector.memset(windows[1][:], 0.0)
 
         def load_scale_rows(queue, tile, scales, packed):
             words = scales.bitcast(I32)
@@ -80,7 +81,7 @@ def tile_list_trapeze_timing_features_kernel(
                     queue.dma_start(out=tile[32 * q : 32 * q + 4, :, :].bitcast(I32), in_=rows.rearrange("a r c -> r a c"))
 
         w2_raw = [late.tile([P, 2, 1024], U8, name="w2_raw%d" % b, align_bytes=64) for b in range(2)]
-        tab2_w = [late.tile([P, TB], I32, name="tab2_w%d" % a, align_bytes=64) for a in range(2)]
+        tab2_w = [late.tile([P, TB], I32, name="tab2_w%d" % a, tag="tab2_w%d" % a, align_bytes=64) for a in range(2)]
         tab_w = last.tile([P, T], I32, name="tab_w", tag="tab_w", align_bytes=64)
         w1_raw = [late.tile([P, 4, 512], F32, name="w1_raw0"), last.tile([P, 4, 512], F32, name="w1_raw1", tag="w1_raw1", align_bytes=64)]
         wg = [late.tile([P, 2, PM], F32, name="wg0"), last.tile([P, 2, PM], F32, name="wg1")]
@@ -121,7 +122,7 @@ def tile_list_trapeze_timing_features_kernel(
         w2_s = []
 
         def deal_w2(b):
-            w2_s.append(held([P, 2, 512], U8, "w2_s%d" % b, after=("tab2_s", "offset0")[b]))
+            w2_s.append(late.tile([P, 2, 512], U8, name="w2_s%d" % b, tag="tab2_w%d" % b, align_bytes=64))
             nc.scalar.copy(
                 out=w2_d[b][:].bitcast(U16).rearrange("p a (t c i) -> p a c t i", t=4, i=8),
                 in_=w2_raw[b][:].bitcast(U16).rearrange("p a (c i t) -> p a c t i", t=4, i=8),
@@ -186,16 +187,17 @@ def tile_list_trapeze_timing_features_kernel(
 
         timing_offsets(0)
         scatter(0)
+        timing_offsets(1)
         round_w1(0)
         deal_w2(1)
-        for i in range(1, 3):
-            timing_offsets(i)
+        scatter(1)
+        timing_offsets(2)
         nc.vector.tensor_copy(out=v_s[:], in_=tab_s[:].indirect(idx[:]))
         quantize_w1(0)
         for h in range(2):
             nc.vector.tensor_copy(out=v[h][:].bitcast(U32), in_=tab_w[:].bitcast(U32).indirect(idx[:, 32 * h : 32 * h + 32]))
-        windows.append(last.tile([P, S], F32, name="window1", tag="tab_w", align_bytes=64))
-        nc.gpsimd.memset(windows[1][:], 0.0)
+        windows.append(last.tile([P, S], F32, name="window2", tag="tab_w", align_bytes=64))
+        nc.gpsimd.memset(windows[2][:], 0.0)
 
         def deal_w3():
             w3_d = last.tile([P, 2, 512], I32, name="w3_d", tag="w1_raw1", align_bytes=64)
@@ -213,7 +215,7 @@ def tile_list_trapeze_timing_features_kernel(
         halves = [(0, HALF), (HALF, HALF)]
         pieces = [(0, QUART), (QUART, QUART), (2 * QUART, QUART), (3 * QUART, EIGHTH), (3 * QUART + EIGHTH, EIGHTH)]
         spans = (halves, pieces)
-        z_rows = [[held([P, 4, w], BF16, "z_rows%d_%d" % (b, j0)) for j0, w in spans[b]] for b in range(2)]
+        z_rows = [held([P, S // EIGHTH, 4, EIGHTH], BF16, "z_rows%d" % b) for b in range(2)]
         z_q = [[held([P, w], I32, "z_q%d_%d" % (b, j0)) for j0, w in spans[b]] for b in range(2)]
         z_s = [[held([P, w], U8, "z_s%d_%d" % (b, j0)) for j0, w in spans[b]] for b in range(2)]
         sines = {}
@@ -222,6 +224,7 @@ def tile_list_trapeze_timing_features_kernel(
             b, t = divmod(i, 4)
             step = QUART if i == 7 else HALF
             xs = []
+            sines[i] = ring.tile([P, S], F32, name="sine", tag="sine", bufs=3)
             for h in range(2):
                 acc = bank([P, HALF], 4 + (2 * i + h) % 4)
                 nc.tensor.matmul_mx(
@@ -230,7 +233,7 @@ def tile_list_trapeze_timing_features_kernel(
                     rhs=v[h][:].bitcast(FP8X4), rhs_scale=v_s[:, HALF * h : HALF * h + HALF], start=True, stop=True,
                 )
                 for c0 in range(0, HALF, step):
-                    x = ring.tile([P, step], F32, name="x", tag="x", bufs=4)
+                    x = ring.tile([P, step], F32, name="x", tag="x%d" % step, bufs=HALF * 2 // step)
                     j0 = HALF * h + c0
                     nc.vector.scalar_tensor_tensor(
                         out=x[:], in0=windows[i % WINDOWS][:, j0 : j0 + step], scalar=inv_gz[:, i : i + 1],
@@ -249,26 +252,23 @@ def tile_list_trapeze_timing_features_kernel(
                     nc.scalar.activation(out=g[:], in_=f[:], func=ACT.Abs, bias=neg_pi[:])
                     twice.append(g)
                 for (j0, x), g in zip(two, twice):
-                    s = ring.tile([P, step], F32, name="sine", tag="sine", bufs=6)
-                    nc.scalar.activation(out=s[:], in_=g[:], func=ACT.Sin, bias=neg_half_pi[:])
-                    sines[(i, j0 // step)] = s
+                    nc.scalar.activation(out=sines[i][:, j0 : j0 + step], in_=g[:], func=ACT.Sin, bias=neg_half_pi[:])
 
-        def finish(i, c):
+        def finish(i, j0, w):
             b, t = divmod(i, 4)
-            j0, w = spans[b][c]
-            n, c0 = divmod(j0, QUART if i == 7 else HALF)
             nc.vector.scalar_tensor_tensor(
-                out=z_rows[b][c][:, t, :], in0=sines[(i, n)][:, c0 : c0 + w], scalar=gz8[:, i : i + 1],
-                in1=windows[i % WINDOWS][:, j0 : j0 + w], op0=ALU.mult, op1=ALU.add,
+                out=z_rows[b][:, j0 // EIGHTH : (j0 + w) // EIGHTH, t, :],
+                in0=sines[i][:, j0 : j0 + w].rearrange("p (e c) -> p e c", c=EIGHTH), scalar=gz8[:, i : i + 1],
+                in1=windows[i % WINDOWS][:, j0 : j0 + w].rearrange("p (e c) -> p e c", c=EIGHTH), op0=ALU.mult, op1=ALU.add,
             )
 
-        def weave(copy, rows, w, tag):
-            woven = ring.tile([P, 4 * w], BF16, name=tag, tag=tag, bufs=3, align_bytes=64)
-            copy(out=woven[:].rearrange("p (c i t) -> p c t i", t=4, i=4), in_=rows[:].rearrange("p t (c i) -> p c t i", i=4))
-            return woven
-
         def quantize_z(b, c, copy):
-            woven = weave(copy, z_rows[b][c], spans[b][c][1], "z_woven")
+            j0, w = spans[b][c]
+            woven = ring.tile([P, 4 * w], BF16, name="z_woven", tag="z_woven", bufs=3, align_bytes=64)
+            copy(
+                out=woven[:].rearrange("p (e c i t) -> p e c t i", c=EIGHTH // 4, t=4, i=4),
+                in_=z_rows[b][:, j0 // EIGHTH : (j0 + w) // EIGHTH, :, :].rearrange("p e t (c i) -> p e c t i", i=4),
+            )
             nc.vector.quantize_mx(out=z_q[b][c][:].bitcast(FP8X4), scales=z_s[b][c][:], in_=woven[:])
 
         y_banks = {}
@@ -299,17 +299,20 @@ def tile_list_trapeze_timing_features_kernel(
             for u in range(4 // per_bank):
                 nc.scalar.copy(out=y[:, per_bank * u : per_bank * u + per_bank, :], in_=y_banks[(c, u)][:])
             nc.sync.dma_start(out=out_rows[:, :, j0 : j0 + w], in_=y[:])
-            woven = weave(copy, y, w, "y_woven")
+            woven = ring.tile([P, 4 * w], BF16, name="y_woven", tag="y_woven", bufs=3, align_bytes=64)
+            copy(out=woven[:].rearrange("p (c i t) -> p c t i", t=4, i=4), in_=y[:].rearrange("p t (c i) -> p c t i", i=4))
             y_q = held([P, w], I32, "y_q%d" % c)
             nc.vector.quantize_mx(out=y_q[:].bitcast(FP8X4), scales=y_s[:, j0 : j0 + w], in_=woven[:])
             nc.sync.dma_start(out=out_words[:, j0 : j0 + w], in_=y_q[:])
 
-        for i in range(8):
+        phases(0)
+        scatter(2)
+        timing_offsets(3)
+        for i in range(1, 8):
+            if i >= 2:
+                finish(i - 2, 0, S)
             phases(i)
-            if i >= 1:
-                for c in range(len(z_rows[(i - 1) // 4])):
-                    finish(i - 1, c)
-            if i + 1 < 8:
+            if 2 <= i < 7:
                 scatter(i + 1)
             if i == 1:
                 round_w1(1)
@@ -317,17 +320,17 @@ def tile_list_trapeze_timing_features_kernel(
                 quantize_w1(1)
             if i + 3 < 8:
                 timing_offsets(i + 3)
-            if i == 4:
+            if i == 5:
                 for h in range(2):
                     quantize_z(0, h, nc.scalar.copy)
-            if i == 5:
                 w3_d, w3_s = deal_w3()
                 for q in range(2):
                     y_pass(0, q)
+        finish(6, 0, S)
         for c in range(2, len(pieces)):
             y_pass(0, c)
         for c in range(len(pieces)):
-            finish(7, c)
+            finish(7, *pieces[c])
             quantize_z(1, c, nc.scalar.copy if c == 1 else nc.vector.tensor_copy)
             y_pass(1, c)
         for c in range(len(pieces)):

import math
from contextlib import ExitStack

import concourse.mybir as mybir

F32 = mybir.dt.float32
BF16 = mybir.dt.bfloat16
I32 = mybir.dt.int32
U32 = mybir.dt.uint32
U16 = mybir.dt.uint16
U8 = mybir.dt.uint8
FP8X4 = mybir.dt.float8_e4m3fn_x4
FP4X4 = mybir.dt.float4_e2m1fn_x4
ALU = mybir.AluOpType
ACT = mybir.ActivationFunctionType

P = 128
T, TB, S, PM = 4096, 2048, 1024, 512
FLOPS = 3221225472
WINDOWS = 3
HALF = 512
QUART = 256
EIGHTH = 128


def tile_list_trapeze_timing_features_kernel(
    tc, tab_words, tab_scales, tab2_words, tab2_scales, offs, offs2, pos1, w1, w2_words, w2_scales,
    gain, wgs, gz, w3_words, w3_scales, out_0, out_1, out_2,
):
    nc = tc.nc
    with ExitStack() as ctx:
        lists = ctx.enter_context(tc.tile_pool(name="lists", bufs=1))
        keep = ctx.enter_context(tc.tile_pool(name="keep", bufs=1))
        ring = ctx.enter_context(tc.tile_pool(name="ring", bufs=3))
        psum = ctx.enter_context(tc.psum_pool(name="psum", bufs=1))

        def held(shape, dtype, name, after=""):
            return keep.tile(shape, dtype, name=name, tag=after or name, align_bytes=64)

        def bank(shape, k):
            return psum.tile(shape, F32, name="bank%d" % k, tag="bank%d" % k)

        idx = lists.tile([P, S // 16], U16, name="idx")
        idx2 = lists.tile([P, PM // 16], U16, name="idx2")
        place = lists.tile([P, PM // 16], U16, name="place")

        tab2_s = held([P, 2, TB], U8, "tab2_s")
        w2_s_raw = held([P, 2, 1024], U8, "w2_s_raw")
        tab_s = held([P, T], U8, "tab_s")
        w3_s_raw = held([P, 512], U8, "w3_s_raw")
        neg_half_pi = held([P, 1], F32, "neg_half_pi")
        neg_pi = held([P, 1], F32, "neg_pi")

        def constant(tile, value, name):
            with tc.tile_pool(name=name, bufs=1) as early:
                ones = early.tile([P, 1], F32, name="ones")
                nc.vector.memset(ones[:], 1.0)
                nc.vector.tensor_scalar(out=tile[:], in0=ones[:], scalar1=value, scalar2=None, op0=ALU.mult)

        nc.gpsimd.memset(w2_s_raw[:].bitcast(I32), 0)
        nc.vector.memset(tab2_s[:].bitcast(I32), 0)
        constant(neg_half_pi, -math.pi / 2, "early")
        late = ctx.enter_context(tc.tile_pool(name="late", bufs=1))
        nc.vector.memset(tab_s[:].bitcast(I32), 0)
        constant(neg_pi, -math.pi, "early2")
        last = ctx.enter_context(tc.tile_pool(name="last", bufs=1))
        windows = [held([P, S], F32, "window0"), held([P, S], F32, "window1")]
        nc.vector.memset(windows[0][:], 0.0)
        nc.vector.memset(windows[1][:], 0.0)

        def load_scale_rows(queue, tile, scales, packed):
            words = scales.bitcast(I32)
            passes = scales.shape[0]
            for q in range(4):
                rows = words[:, 4 * q : 4 * q + 4, :]
                if packed:
                    queue.dma_start(out=tile[32 * q : 32 * q + 4 * passes, :].bitcast(I32), in_=rows)
                elif passes == 1:
                    queue.dma_start(out=tile[32 * q : 32 * q + 4, :].bitcast(I32), in_=rows[0])
                else:
                    queue.dma_start(out=tile[32 * q : 32 * q + 4, :, :].bitcast(I32), in_=rows.rearrange("a r c -> r a c"))

        w2_raw = [late.tile([P, 2, 1024], U8, name="w2_raw%d" % b, align_bytes=64) for b in range(2)]
        tab2_w = [late.tile([P, TB], I32, name="tab2_w%d" % a, tag="tab2_w%d" % a, align_bytes=64) for a in range(2)]
        tab_w = last.tile([P, T], I32, name="tab_w", tag="tab_w", align_bytes=64)
        w1_raw = [late.tile([P, 4, 512], F32, name="w1_raw0"), last.tile([P, 4, 512], F32, name="w1_raw1", tag="w1_raw1", align_bytes=64)]
        wg = [late.tile([P, 2, PM], F32, name="wg0"), last.tile([P, 2, PM], F32, name="wg1")]
        w3_raw = last.tile([P, 2, 512], I32, name="w3_raw")
        gain_sb = late.tile([P, 2, 4], F32, name="gain_sb")
        gz_sb = late.tile([P, 2, 4], F32, name="gz_sb")
        w1_rows = w1.rearrange("(p j) r -> p j r", j=4)
        wgs_rows = wgs.rearrange("(i t) j -> i t j", t=4)

        def load_wgs(u):
            for q in (0, 2, 1, 3):
                nc.sync.dma_start(out=wg[u][32 * q : 32 * q + 32, :, :], in_=wgs_rows[:, 2 * u : 2 * u + 2, :])

        nc.sync.dma_start(out=idx2[:], in_=offs2)
        nc.sync.dma_start(out=place[:], in_=pos1)
        nc.sync.dma_start(out=idx[:], in_=offs)
        load_scale_rows(nc.scalar, tab2_s, tab2_scales, False)
        load_scale_rows(nc.gpsimd, w2_s_raw, w2_scales, False)
        nc.gpsimd.memset(w3_s_raw[:].bitcast(I32), 0)
        load_scale_rows(nc.gpsimd, w3_s_raw, w3_scales, True)
        w2_rows = w2_words.bitcast(I32).rearrange("a p c -> p a c")
        nc.sync.dma_start(out=tab2_w[0][:], in_=tab2_words[0].rearrange("p t i -> p (t i)").bitcast(I32))
        nc.sync.dma_start(out=w2_raw[0][:].bitcast(I32), in_=w2_rows[:, :, 0:256])
        nc.sync.dma_start(out=tab2_w[1][:], in_=tab2_words[1].rearrange("p t i -> p (t i)").bitcast(I32))
        nc.sync.dma_start(out=gain_sb[:], in_=gain.rearrange("(b p t) -> p b t", b=2, t=4))
        nc.sync.dma_start(out=gz_sb[:], in_=gz.rearrange("(b p t) -> p b t", b=2, t=4))
        load_wgs(0)
        nc.sync.dma_start(out=w1_raw[0][:], in_=w1_rows[:, :, 0:512])
        nc.sync.dma_start(out=w2_raw[1][:].bitcast(I32), in_=w2_rows[:, :, 256:512])
        load_scale_rows(nc.sync, tab_s, tab_scales, False)
        nc.sync.dma_start(out=tab_w[:], in_=tab_words[0].rearrange("p t i -> p (t i)").bitcast(I32))
        load_wgs(1)
        nc.sync.dma_start(out=w1_raw[1][:], in_=w1_rows[:, :, 512:1024])
        nc.sync.dma_start(out=w3_raw[:], in_=w3_words.rearrange("a p n i -> p a (n i)").bitcast(I32))


        w2_d = [held([P, 2, 1024], U8, "w2_d%d" % b) for b in range(2)]
        w2_s = []

        def deal_w2(b):
            w2_s.append(late.tile([P, 2, 512], U8, name="w2_s%d" % b, tag="tab2_w%d" % b, align_bytes=64))
            nc.scalar.copy(
                out=w2_d[b][:].bitcast(U16).rearrange("p a (t c i) -> p a c t i", t=4, i=8),
                in_=w2_raw[b][:].bitcast(U16).rearrange("p a (c i t) -> p a c t i", t=4, i=8),
            )
            nc.vector.tensor_copy(
                out=w2_s[b][:].rearrange("p a (t c i) -> p a c t i", t=4, i=16),
                in_=w2_s_raw[:, :, 512 * b : 512 * b + 512].rearrange("p a (c i t) -> p a c t i", t=4, i=16),
            )

        v2 = [held([P, PM], I32, "v2_%d" % a) for a in range(2)]
        v2_s = held([P, 2, PM], U8, "v2_s")
        for a in range(2):
            nc.vector.tensor_copy(out=v2_s[:, a, :], in_=tab2_s[:, a, :].indirect(idx2[:]))
        nc.vector.tensor_copy(out=v2[0][:].bitcast(U32), in_=tab2_w[0][:].bitcast(U32).indirect(idx2[:]))
        deal_w2(0)

        gz8 = gz_sb[:].rearrange("p b t -> p (b t)")
        gain_gz = held([P, 8], F32, "gain_gz")
        safe_gz = held([P, 8], F32, "safe_gz")
        inv_gz = held([P, 8], F32, "inv_gz")
        nc.vector.tensor_tensor(out=gain_gz[:], in0=gain_sb[:].rearrange("p b t -> p (b t)"), in1=gz8, op=ALU.mult)
        nc.vector.scalar_tensor_tensor(out=safe_gz[:], in0=gz8, scalar=0.0, in1=gz8, op0=ALU.is_equal, op1=ALU.add)
        nc.vector.tensor_copy(out=v2[1][:].bitcast(U32), in_=tab2_w[1][:].bitcast(U32).indirect(idx2[:]))
        nc.vector.reciprocal(out=inv_gz[:], in_=safe_gz[:])

        offsets = []

        def timing_offsets(i):
            b, t = divmod(i, 4)
            acc = bank([P, PM], i % 4)
            for a in range(2):
                nc.tensor.matmul_mx(
                    out=acc[:], lhsT=w2_d[b][:, a, 256 * t : 256 * t + 256].bitcast(FP4X4),
                    lhsT_scale=w2_s[b][:, a, 128 * t : 128 * t + 128],
                    rhs=v2[a][:].bitcast(FP8X4), rhs_scale=v2_s[:, a, :], start=(a == 0), stop=(a == 1),
                )
            scaled = held([P, PM], F32, "offset%d" % i, after="offset%d" % (0, 1, 2, 3, 1, 2, 3, 1)[i])
            nc.scalar.activation(out=scaled[:], in_=acc[:], func=ACT.Copy, scale=gain_gz[:, i : i + 1])
            offsets.append(scaled)

        def scatter(i):
            t = i % 4
            nc.vector.tensor_tensor(
                out=windows[i % WINDOWS][:].indirect(place[:]), in0=offsets[i][:], in1=wg[t // 2][:, t % 2, :], op=ALU.mult
            )

        v_s = held([P, S], U8, "v_s")
        v = [held([P, HALF], I32, "v%d" % h) for h in range(2)]
        w1_q = [held([P, 512], I32, "w1_q%d" % b) for b in range(2)]
        w1_s = [held([P, 512], U8, "w1_s%d" % b) for b in range(2)]
        w1_bf = []

        def round_w1(b):
            w1_bf.append(held([P, 2048], BF16, "w1_bf%d" % b, after="offset2" if b == 1 else ""))
            nc.scalar.copy(
                out=w1_bf[b][:].rearrange("p (t m j) -> p m t j", t=4, j=4),
                in_=w1_raw[b][:].rearrange("p j (m t) -> p m t j", t=4),
            )

        def quantize_w1(b):
            nc.vector.quantize_mx(out=w1_q[b][:].bitcast(FP8X4), scales=w1_s[b][:], in_=w1_bf[b][:])

        timing_offsets(0)
        scatter(0)
        timing_offsets(1)
        round_w1(0)
        deal_w2(1)
        scatter(1)
        timing_offsets(2)
        nc.vector.tensor_copy(out=v_s[:], in_=tab_s[:].indirect(idx[:]))
        quantize_w1(0)
        for h in range(2):
            nc.vector.tensor_copy(out=v[h][:].bitcast(U32), in_=tab_w[:].bitcast(U32).indirect(idx[:, 32 * h : 32 * h + 32]))
        windows.append(last.tile([P, S], F32, name="window2", tag="tab_w", align_bytes=64))
        nc.gpsimd.memset(windows[2][:], 0.0)

        def deal_w3():
            w3_d = last.tile([P, 2, 512], I32, name="w3_d", tag="w1_raw1", align_bytes=64)
            w3_s = held([P, 512], U8, "w3_s", after="offset3")
            nc.scalar.copy(
                out=w3_d[:].bitcast(U32).rearrange("p a (t c i) -> p a c t i", t=4, i=4),
                in_=w3_raw[:].bitcast(U32).rearrange("p a (c i t) -> p a c t i", t=4, i=4),
            )
            nc.vector.tensor_copy(
                out=w3_s[:].rearrange("p (t c i) -> p c t i", t=4, i=16),
                in_=w3_s_raw[:].rearrange("p (c i t) -> p c t i", t=4, i=16),
            )
            return w3_d, w3_s

        halves = [(0, HALF), (HALF, HALF)]
        pieces = [(0, QUART), (QUART, QUART), (2 * QUART, QUART), (3 * QUART, EIGHTH), (3 * QUART + EIGHTH, EIGHTH)]
        spans = (halves, pieces)
        z_rows = [held([P, S // EIGHTH, 4, EIGHTH], BF16, "z_rows%d" % b) for b in range(2)]
        z_q = [[held([P, w], I32, "z_q%d_%d" % (b, j0)) for j0, w in spans[b]] for b in range(2)]
        z_s = [[held([P, w], U8, "z_s%d_%d" % (b, j0)) for j0, w in spans[b]] for b in range(2)]
        sines = {}

        def phases(i):
            b, t = divmod(i, 4)
            step = QUART if i == 7 else HALF
            xs = []
            sines[i] = ring.tile([P, S], F32, name="sine", tag="sine", bufs=3)
            for h in range(2):
                acc = bank([P, HALF], 4 + (2 * i + h) % 4)
                nc.tensor.matmul_mx(
                    out=acc[:], lhsT=w1_q[b][:, 128 * t : 128 * t + 128].bitcast(FP8X4),
                    lhsT_scale=w1_s[b][:, 128 * t : 128 * t + 128],
                    rhs=v[h][:].bitcast(FP8X4), rhs_scale=v_s[:, HALF * h : HALF * h + HALF], start=True, stop=True,
                )
                for c0 in range(0, HALF, step):
                    x = ring.tile([P, step], F32, name="x", tag="x%d" % step, bufs=HALF * 2 // step)
                    j0 = HALF * h + c0
                    nc.vector.scalar_tensor_tensor(
                        out=x[:], in0=windows[i % WINDOWS][:, j0 : j0 + step], scalar=inv_gz[:, i : i + 1],
                        in1=acc[:, c0 : c0 + step], op0=ALU.mult, op1=ALU.add,
                    )
                    xs.append((j0, x))
            for pair in range(0, len(xs), 2):
                two = xs[pair : pair + 2]
                once, twice = [], []
                for j0, x in two:
                    f = ring.tile([P, step], F32, name="fold1", tag="fold1", bufs=2)
                    nc.scalar.activation(out=f[:], in_=x[:], func=ACT.Abs, bias=neg_half_pi[:])
                    once.append(f)
                for f in once:
                    g = ring.tile([P, step], F32, name="fold2", tag="fold2", bufs=2)
                    nc.scalar.activation(out=g[:], in_=f[:], func=ACT.Abs, bias=neg_pi[:])
                    twice.append(g)
                for (j0, x), g in zip(two, twice):
                    nc.scalar.activation(out=sines[i][:, j0 : j0 + step], in_=g[:], func=ACT.Sin, bias=neg_half_pi[:])

        def finish(i, j0, w):
            b, t = divmod(i, 4)
            nc.vector.scalar_tensor_tensor(
                out=z_rows[b][:, j0 // EIGHTH : (j0 + w) // EIGHTH, t, :],
                in0=sines[i][:, j0 : j0 + w].rearrange("p (e c) -> p e c", c=EIGHTH), scalar=gz8[:, i : i + 1],
                in1=windows[i % WINDOWS][:, j0 : j0 + w].rearrange("p (e c) -> p e c", c=EIGHTH), op0=ALU.mult, op1=ALU.add,
            )

        def quantize_z(b, c, copy):
            j0, w = spans[b][c]
            woven = ring.tile([P, 4 * w], BF16, name="z_woven", tag="z_woven", bufs=3, align_bytes=64)
            copy(
                out=woven[:].rearrange("p (e c i t) -> p e c t i", c=EIGHTH // 4, t=4, i=4),
                in_=z_rows[b][:, j0 // EIGHTH : (j0 + w) // EIGHTH, :, :].rearrange("p e t (c i) -> p e c t i", i=4),
            )
            nc.vector.quantize_mx(out=z_q[b][c][:].bitcast(FP8X4), scales=z_s[b][c][:], in_=woven[:])

        y_banks = {}

        def y_pass(a, c):
            j0, w = pieces[c]
            per_bank = 512 // w
            n, c0 = (c, 0) if a == 1 else divmod(j0, HALF)
            for t in range(4):
                u, slot = divmod(t, per_bank)
                if a == 0 and slot == 0:
                    y_banks[(c, u)] = bank([P, per_bank, w], j0 // EIGHTH + u)
                nc.tensor.matmul_mx(
                    out=y_banks[(c, u)][:, slot, :], lhsT=w3_d[:, a, 128 * t : 128 * t + 128].bitcast(FP8X4),
                    lhsT_scale=w3_s[4 * a : 128, 128 * t : 128 * t + 128],
                    rhs=z_q[a][n][:, c0 : c0 + w].bitcast(FP8X4), rhs_scale=z_s[a][n][:, c0 : c0 + w],
                    start=(a == 0 and slot == 0), stop=(a == 1 and slot == per_bank - 1),
                )

        y_s = held([P, S], U8, "y_s")
        out_rows = out_0.rearrange("(p t) j -> p t j", t=4)
        out_words = out_1[0].rearrange("p m t -> p (m t)").bitcast(I32)

        def hand_out(c, copy):
            j0, w = pieces[c]
            per_bank = 512 // w
            y = held([P, 4, w], F32, "y%d" % c)
            for u in range(4 // per_bank):
                nc.scalar.copy(out=y[:, per_bank * u : per_bank * u + per_bank, :], in_=y_banks[(c, u)][:])
            nc.sync.dma_start(out=out_rows[:, :, j0 : j0 + w], in_=y[:])
            woven = ring.tile([P, 4 * w], BF16, name="y_woven", tag="y_woven", bufs=3, align_bytes=64)
            copy(out=woven[:].rearrange("p (c i t) -> p c t i", t=4, i=4), in_=y[:].rearrange("p t (c i) -> p c t i", i=4))
            y_q = held([P, w], I32, "y_q%d" % c)
            nc.vector.quantize_mx(out=y_q[:].bitcast(FP8X4), scales=y_s[:, j0 : j0 + w], in_=woven[:])
            nc.sync.dma_start(out=out_words[:, j0 : j0 + w], in_=y_q[:])

        phases(0)
        scatter(2)
        timing_offsets(3)
        for i in range(1, 8):
            if i >= 2:
                finish(i - 2, 0, S)
            phases(i)
            if 2 <= i < 7:
                scatter(i + 1)
            if i == 1:
                round_w1(1)
            if i == 2:
                quantize_w1(1)
            if i + 3 < 8:
                timing_offsets(i + 3)
            if i == 5:
                for h in range(2):
                    quantize_z(0, h, nc.scalar.copy)
                w3_d, w3_s = deal_w3()
                for q in range(2):
                    y_pass(0, q)
        finish(6, 0, S)
        for c in range(2, len(pieces)):
            y_pass(0, c)
        for c in range(len(pieces)):
            finish(7, *pieces[c])
            quantize_z(1, c, nc.scalar.copy if c == 1 else nc.vector.tensor_copy)
            y_pass(1, c)
        for c in range(len(pieces)):
            hand_out(c, nc.scalar.copy if c == 0 else nc.vector.tensor_copy)
        scale_words = out_2[0].bitcast(I32)
        for q in range(4):
            nc.sync.dma_start(out=scale_words[4 * q : 4 * q + 4, :], in_=y_s[32 * q : 32 * q + 4, :].bitcast(I32))
